import numpy as np
import ml_dtypes


def mxq(x, axis, fmt="e4m3"):
    dtype, down = {"e4m3": (ml_dtypes.float8_e4m3fn, 7), "e5m2": (ml_dtypes.float8_e5m2, 14)}[fmt]
    v = np.moveaxis(np.asarray(x, np.float32).astype(ml_dtypes.bfloat16).astype(np.float64), axis, -1)
    blocks = v.reshape(v.shape[:-1] + (-1, 32))
    amax = np.abs(blocks).max(-1, keepdims=True)
    byte = np.maximum(np.where(amax > 0, np.frexp(amax)[1] - 1 + 127, 0) - down, 1)
    scale = np.exp2(byte - 127.0)
    codes = (blocks / scale).astype(np.float32).astype(dtype).astype(np.float64)
    return np.moveaxis((codes * scale).reshape(v.shape), -1, axis)


WIDE = False


def mx_kscale(k):
    if not WIDE:
        return np.ones(k)
    levels = np.array([10, -10, 5, -5, 0])
    if k % 512:
        return np.exp2(np.random.permutation(np.resize(levels, k // 32))).repeat(32)
    a = np.empty((k // 512, 16))
    for p in range(k // 512):
        a[p, :8] = np.random.permutation(np.resize(levels, 8))
        for g in range(8):
            far = levels[np.abs(levels - a[p, g]) >= 10]
            a[p, g + 8] = far[np.random.randint(len(far))]
    return np.exp2(a.ravel()).repeat(32)


def f64(x):
    return np.asarray(x).astype(np.float64)


def striped(idx):
    return np.tile(np.asarray(idx).reshape(-1, 16).T, (8, 1)).astype(np.uint16)


def unstriped(offs):
    return offs[:16].T.reshape(-1).astype(np.int64)


E2M1 = np.array([0.0, 0.5, 1.0, 1.5, 2.0, 3.0, 4.0, 6.0, -0.0, -0.5, -1.0, -1.5, -2.0, -3.0, -4.0, -6.0])


def pack_weight(w, fmt):
    k, n = w.shape
    w = f64(np.asarray(w, np.float32).astype(ml_dtypes.bfloat16)).reshape(k // 32, 32, n)
    amax = np.abs(w).max(1)
    if fmt == "e4m3":
        byte = np.frexp(amax)[1] - 1 + 127 - 7
    else:
        mant, ex = np.frexp(amax / 6.0)
        byte = np.where(mant > 0.5, ex, ex - 1) + 127
    byte = np.clip(np.where(amax > 0, byte, 1), 1, 254)
    scaled = (w * np.exp2(127.0 - byte)[:, None, :]).reshape(k, n).astype(np.float32)
    by_word = np.ascontiguousarray(scaled.reshape(k // 512, 128, 4, n).transpose(0, 1, 3, 2))
    if fmt == "e4m3":
        words = by_word.astype(ml_dtypes.float8_e4m3fn).view(np.uint8)
    else:
        c = by_word.astype(ml_dtypes.float4_e2m1fn).view(np.uint8) & 0xF
        words = (c[..., 0::2] | (c[..., 1::2] << 4)).reshape(k // 512, 128, 2 * n)
    return np.ascontiguousarray(words), np.ascontiguousarray(byte.astype(np.uint8).reshape(k // 512, 16, n))


def unpack_weight(words, scales, fmt):
    g, _, n = scales.shape
    words = np.ascontiguousarray(words).reshape(g, 128, n, -1)
    if fmt == "e4m3":
        vals = words.view(ml_dtypes.float8_e4m3fn).astype(np.float64)
    else:
        nib = np.empty((g, 128, n, 4), np.uint8)
        nib[..., 0::2] = words & 0xF
        nib[..., 1::2] = words >> 4
        vals = E2M1[nib]
    vals = vals * np.repeat(np.exp2(scales.astype(np.float64) - 127.0), 8, axis=1)[..., None]
    return vals.transpose(0, 1, 3, 2).reshape(g * 512, n)


def bf(x):
    return np.asarray(x, np.float32).astype(ml_dtypes.bfloat16)


def planes(Y):
    r, m = Y.shape
    b = f64(bf(Y)).reshape(r // 32, 32, m)
    amax = np.abs(b).max(1)
    byte = np.clip(np.where(amax > 0, np.frexp(amax)[1] - 1 + 127 - 7, 1), 1, 254)
    codes = (b * np.exp2(127.0 - byte)[:, None, :]).reshape(r, m).astype(np.float32).astype(ml_dtypes.float8_e4m3fn).view(np.uint8)
    words = codes.reshape(r // 512, 128, 4, m).transpose(0, 1, 3, 2)
    return np.ascontiguousarray(words), np.ascontiguousarray(byte.astype(np.uint8).reshape(r // 512, 16, m))


D, T, I, Q, E, U = 512, 2048, 512, 256, 512, 512


def setup_inputs():
    n = np.random.standard_normal
    idx = np.random.permutation(T)[:I]
    idx2 = np.random.randint(0, U, I)
    fd = mx_kscale(D)
    fi = mx_kscale(I)
    ti = np.ones(T)
    ti[idx] = fi
    remp = pack_weight(n((D, T)) * 0.7 / fd[:, None], "e2m1")
    return {
        "query": (n((D, Q)) * 0.25 / np.sqrt(D) * fd[:, None]).astype(np.float32),
        "cent": (n((D, U)) / fd[:, None]).astype(np.float32),
        "rem_words": remp[0],
        "rem_scales": remp[1],
        "size": (np.random.uniform(0.5, 2.0, (1, I)) * fi).astype(np.float32),
        "vals": (n((E, T)) / ti).astype(np.float32),
        "offs": striped(idx),
        "offs2": striped(idx2),
    }


def reference(query, cent, rem_words, rem_scales, size, vals, offs, offs2):
    idx = unstriped(offs)
    idx2 = unstriped(offs2)
    remu = unpack_weight(rem_words, rem_scales, "e2m1")
    queryq = mxq(f64(query), 0, "e4m3")
    centq = mxq(f64(cent), 0, "e4m3")
    c1 = queryq.T @ centq
    remidxg = remu[:, idx]
    b = queryq.T @ remidxg
    s = c1[:, idx2] + b
    p = np.exp(s - np.max(s, axis=1, keepdims=True))
    w = p * f64(size) / np.sum(p, axis=1, keepdims=True)
    wt = w.T
    vt = f64(vals)[:, idx].T
    vtq = mxq(vt, 0, "e4m3")
    wtq = mxq(wt, 0, "e4m3")
    o = vtq.T @ wtq
    words, scales = planes(o)
    return o, words, scales

@@ -1,0 +1,179 @@
+from contextlib import ExitStack
+
+import concourse.mybir as mybir
+from concourse.masks import make_identity
+
+D, T, I, Q, E, U = 512, 2048, 512, 256, 512, 512
+FLOPS = 2 * D * Q * U + 2 * D * Q * I + 2 * I * E * Q
+
+F32 = mybir.dt.float32
+BF16 = mybir.dt.bfloat16
+I32 = mybir.dt.int32
+U32 = mybir.dt.uint32
+U16 = mybir.dt.uint16
+U8 = mybir.dt.uint8
+FP8X4 = mybir.dt.float8_e4m3fn_x4
+FP4X4 = mybir.dt.float4_e2m1fn_x4
+ALU = mybir.AluOpType
+ACT = mybir.ActivationFunctionType
+
+P = 128
+PACK = 4
+QT = Q // P
+CH = 2
+UC = U // CH
+SPARE = 16
+
+
+def tile_attend_centreremainder_pl_kernel(tc, query, cent, rem_words, rem_scales, size, vals, offs, offs2, out_0, out_1, out_2):
+    nc = tc.nc
+    with ExitStack() as ctx:
+        sb = ctx.enter_context(tc.tile_pool(name="sb", bufs=1))
+        ps = ctx.enter_context(tc.psum_pool(name="ps", bufs=1))
+
+        def sbt(name, shape, dt, tag=None):
+            return sb.tile(shape, dt, name=name, tag=tag or name, align_bytes=64)
+
+        slots = sbt("slots", [P, I // 16], U16)
+        centres = sbt("centres", [P, I // 16], U16)
+        bank = [ps.tile([P, 512], F32, name="bank%d" % b) for b in range(8)]
+
+        rem_w = sbt("rem_w", [P, T], U16)
+        rem_s = sbt("rem_s", [P, T], U8)
+        q_raw = sbt("q_raw", [P, PACK, Q], F32)
+        c_raw = [sbt("c_raw%d" % h, [P, PACK, UC], F32) for h in range(CH)]
+        size4 = sbt("size4", [P, PACK], F32)
+        v_raw = [sbt("v_raw%d" % j, [P, T], F32) for j in range(PACK)]
+        c1 = [sbt("c1_%d" % h, [P, U + SPARE], F32) for h in range(QT)]
+        ident = sbt("ident", [P, P], F32)
+
+        nc.gpsimd.memset(rem_s[:].bitcast(I32), 0)
+        nc.sync.dma_start(slots[:], offs)
+        nc.sync.dma_start(q_raw[:], query.rearrange("(p j) q -> p j q", j=PACK))
+        nc.sync.dma_start(centres[:], offs2)
+        nc.sync.dma_start(size4[:], size.rearrange("o (p t) -> p (o t)", t=PACK))
+        for g in range(4):
+            nc.sync.dma_start(rem_s[32 * g : 32 * g + 4, :].bitcast(I32), rem_scales[0, 4 * g : 4 * g + 4, :].bitcast(I32))
+        nc.sync.dma_start(rem_w[:].bitcast(I32), rem_words[0].bitcast(I32))
+        cent_v = cent.rearrange("(p j) u -> p j u", j=PACK)
+        for h in range(CH):
+            nc.sync.dma_start(c_raw[h][:], cent_v[:, :, h * UC : (h + 1) * UC])
+        vals_v = vals.rearrange("(p j) t -> j p t", j=PACK)
+        for j in range(PACK):
+            nc.sync.dma_start(v_raw[j][:], vals_v[j])
+
+        make_identity(nc, ident[:])
+        for h in range(QT):
+            nc.gpsimd.memset(c1[h][:, U:], 0.0)
+
+        def weave(copy, name, raw, width):
+            woven = sbt(name, [P, width, PACK], BF16)
+            copy(woven[:].rearrange("p (c i) t -> p c t i", i=4), raw[:].rearrange("p t (c i) -> p c t i", i=4))
+            return woven[:].rearrange("p c t -> p (c t)")
+
+        def quantise(name, woven, width, tag=None):
+            codes = sbt(name + "_codes", [P, width], U32, tag)
+            scales = sbt(name + "_scales", [P, width], U8)
+            nc.vector.quantize_mx(out=codes[:].bitcast(FP8X4), scales=scales[:], in_=woven)
+            return codes, scales
+
+        def mx(out, lhs, lcols, rhs_codes, rhs_scales):
+            nc.tensor.matmul_mx(out=out, lhsT=lhs[0][:, lcols].bitcast(FP8X4), lhsT_scale=lhs[1][:, lcols],
+                                rhs=rhs_codes, rhs_scale=rhs_scales, start=True, stop=True)
+
+        rem_sg = sbt("rem_sg", [P, I], U8)
+        rem_wg = sbt("rem_wg", [P, I], U16)
+        nc.vector.tensor_copy(rem_sg[:], rem_s[:].indirect(slots[:]))
+        q_mx = quantise("q", weave(nc.scalar.copy, "q_woven", q_raw, Q), Q)
+        nc.vector.tensor_copy(rem_wg[:], rem_w[:].indirect(slots[:]))
+        c_woven = [weave(copy, "c_woven%d" % ch, c_raw[ch], UC) for ch, copy in enumerate((nc.scalar.copy, nc.vector.tensor_copy))]
+
+        b_sb = [sbt("b_sb%d" % h, [P, I], F32) for h in range(QT)]
+        for h in range(QT):
+            mx(bank[4 + h][:], q_mx, slice(h * P, (h + 1) * P), rem_wg[:].bitcast(FP4X4), rem_sg[:])
+            nc.scalar.copy(b_sb[h][:], bank[4 + h][:])
+        for ch in range(CH):
+            c_mx = quantise("c%d" % ch, c_woven[ch], UC)
+            for h in range(QT):
+                mx(bank[2 * ch + h][:, :UC], q_mx, slice(h * P, (h + 1) * P), c_mx[0][:].bitcast(FP8X4), c_mx[1][:])
+                nc.scalar.copy(c1[h][:, ch * UC : (ch + 1) * UC], bank[2 * ch + h][:, :UC])
+
+        size_row = sbt("size_row", [P, I], F32)
+        for t in range(PACK):
+            nc.tensor.transpose(bank[3][:, t * P : (t + 1) * P], size4[:, t : t + 1].to_broadcast([P, P]), ident[:])
+        nc.scalar.copy(size_row[:].rearrange("c (u b r t) -> c u b r t", u=2, b=16, r=4),
+                       bank[3][:].rearrange("c (t b u r) -> c u b r t", t=4, b=16, u=2))
+
+        def turn(name, half_words, bk, tag=None):
+            words = half_words[:].bitcast(F32)
+            for u in range(2):
+                nc.tensor.transpose(bk[:, u * P : (u + 1) * P], words[:, u * P : (u + 1) * P], ident[:])
+            woven = sbt(name + "_woven", [P, P * PACK], BF16)
+            nc.scalar.copy(woven[:].bitcast(F32).rearrange("p (c u) -> p c u", u=2),
+                           bk[:, : 2 * P].rearrange("p (u c) -> p c u", u=2))
+            return quantise(name, woven[:], P, tag)
+
+        s = [sbt("s%d" % h, [P, I], F32) for h in range(QT)]
+        neg_max = [sbt("neg_max%d" % h, [P, 1], F32) for h in range(QT)]
+        p_exp = [sbt("p_exp%d" % h, [P, I], F32) for h in range(QT)]
+        total = sbt("total", [P, QT], F32)
+        inv = sbt("inv", [P, QT], F32)
+        w = [sbt("w%d" % h, [P, I], BF16) for h in range(QT)]
+        vg_tag = ["vg0", "b_sb1", "p_exp0", "vg3"]
+        vg = []
+
+        def gather_values(j):
+            vg.append(sbt("vg%d" % j, [P, I], BF16, vg_tag[j]))
+            nc.vector.tensor_copy(vg[j][:].rearrange("p (u b r) -> p b u r", u=2, b=16), v_raw[j][:].indirect(slots[:]))
+
+        gather_values(0)
+        for h in range(QT):
+            nc.vector.tensor_tensor(s[h][:], c1[h][:].indirect(centres[:]), b_sb[h][:], ALU.add)
+        for h in range(QT):
+            nc.vector.tensor_reduce(neg_max[h][:], s[h][:], mybir.AxisListType.X, ALU.max, negate=True)
+            nc.scalar.activation(p_exp[h][:].rearrange("p (u b r) -> p u b r", u=2, b=16),
+                                 s[h][:].rearrange("p (b u r) -> p u b r", u=2, b=16),
+                                 ACT.Exp, bias=neg_max[h][:], accum_out=total[:, h : h + 1])
+        v_bank = [bank[6], bank[7], bank[2], bank[3]]
+        v_mx = []
+        w_mx = []
+        gather_values(1)
+        nc.vector.reciprocal(inv[:], total[:])
+        v_mx.append(turn("v0", vg[0], v_bank[0], "s1"))
+        for h in range(QT):
+            nc.vector.scalar_tensor_tensor(w[h][:], p_exp[h][:], inv[:, h : h + 1], size_row[:], ALU.mult, ALU.mult)
+        gather_values(2)
+        v_mx.append(turn("v1", vg[1], v_bank[1]))
+        for h in range(QT):
+            w_mx.append(turn("w%d" % h, w[h], bank[4 + h]))
+        gather_values(3)
+
+        o_bank = [bank[h][:].rearrange("p (j q) -> p j q", j=PACK) for h in range(QT)]
+        o_sb = sbt("o_sb", [P, PACK, Q], F32)
+        out_v = out_0.rearrange("(p j) q -> p j q", j=PACK)
+
+        def product(j):
+            for h in range(QT):
+                mx(o_bank[h][:, j, :], v_mx[j], slice(0, P), w_mx[h][0][:].bitcast(FP8X4), w_mx[h][1][:])
+
+        product(0)
+        product(1)
+        for h in range(QT):
+            nc.scalar.copy(o_sb[:, :2, h * P : (h + 1) * P], o_bank[h][:, :2, :])
+        nc.sync.dma_start(out_v[:, :2, :], o_sb[:, :2, :])
+        v_mx.append(turn("v2", vg[2], v_bank[2], "v_raw3"))
+        product(2)
+        v_mx.append(turn("v3", vg[3], v_bank[3]))
+        product(3)
+
+        o_woven = sbt("o_woven", [P, Q, PACK], BF16)
+        nc.scalar.copy(o_woven[:, :P, :], o_bank[0].rearrange("p j q -> p q j"))
+        nc.vector.tensor_copy(o_woven[:, P:, :], o_bank[1].rearrange("p j q -> p q j"))
+        for h in range(QT):
+            nc.scalar.copy(o_sb[:, 2:, h * P : (h + 1) * P], o_bank[h][:, 2:, :])
+        nc.scalar.dma_start(out_v[:, 2:, :], o_sb[:, 2:, :])
+        o_codes, o_scales = quantise("o", o_woven[:].rearrange("p c t -> p (c t)"), Q)
+        nc.sync.dma_start(out_1[0].rearrange("p c t -> p (c t)").bitcast(I32), o_codes[:].bitcast(I32))
+        for g in range(4):
+            eng = nc.sync if g < 2 else nc.scalar
+            eng.dma_start(out_2[0, 4 * g : 4 * g + 4, :].bitcast(I32), o_scales[32 * g : 32 * g + 4, :].bitcast(I32))

@@ -49,15 +49,15 @@ def tile_attend_centreremainder_pl_kernel(tc, query, cent, rem_words, rem_scales
 
         nc.gpsimd.memset(rem_s[:].bitcast(I32), 0)
         nc.sync.dma_start(slots[:], offs)
+        nc.sync.dma_start(rem_w[:].bitcast(I32), rem_words[0].bitcast(I32))
         nc.sync.dma_start(q_raw[:], query.rearrange("(p j) q -> p j q", j=PACK))
-        nc.sync.dma_start(centres[:], offs2)
+        cent_v = cent.rearrange("(p j) u -> p j u", j=PACK)
         nc.sync.dma_start(size4[:], size.rearrange("o (p t) -> p (o t)", t=PACK))
         for g in range(4):
             nc.sync.dma_start(rem_s[32 * g : 32 * g + 4, :].bitcast(I32), rem_scales[0, 4 * g : 4 * g + 4, :].bitcast(I32))
-        nc.sync.dma_start(rem_w[:].bitcast(I32), rem_words[0].bitcast(I32))
-        cent_v = cent.rearrange("(p j) u -> p j u", j=PACK)
-        for h in range(CH):
-            nc.sync.dma_start(c_raw[h][:], cent_v[:, :, h * UC : (h + 1) * UC])
+        nc.sync.dma_start(c_raw[0][:], cent_v[:, :, :UC])
+        nc.sync.dma_start(c_raw[1][:], cent_v[:, :, UC:])
+        nc.sync.dma_start(centres[:], offs2)
         vals_v = vals.rearrange("(p j) t -> j p t", j=PACK)
         for j in range(PACK):
             nc.sync.dma_start(v_raw[j][:], vals_v[j])
@@ -66,13 +66,14 @@ def tile_attend_centreremainder_pl_kernel(tc, query, cent, rem_words, rem_scales
         for h in range(QT):
             nc.gpsimd.memset(c1[h][:, U:], 0.0)
 
-        def weave(copy, name, raw, width):
-            woven = sbt(name, [P, width, PACK], BF16)
+        def weave(copy, name, raw, width, tag=None):
+            woven = sbt(name, [P, width, PACK], BF16, tag)
             copy(woven[:].rearrange("p (c i) t -> p c t i", i=4), raw[:].rearrange("p t (c i) -> p c t i", i=4))
             return woven[:].rearrange("p c t -> p (c t)")
 
-        def quantise(name, woven, width, tag=None):
-            codes = sbt(name + "_codes", [P, width], U32, tag)
+        def quantise(name, woven, width, tag=None, codes=None):
+            if codes is None:
+                codes = sbt(name + "_codes", [P, width], U32, tag)
             scales = sbt(name + "_scales", [P, width], U8)
             nc.vector.quantize_mx(out=codes[:].bitcast(FP8X4), scales=scales[:], in_=woven)
             return codes, scales
@@ -81,99 +82,104 @@ def tile_attend_centreremainder_pl_kernel(tc, query, cent, rem_words, rem_scales
             nc.tensor.matmul_mx(out=out, lhsT=lhs[0][:, lcols].bitcast(FP8X4), lhsT_scale=lhs[1][:, lcols],
                                 rhs=rhs_codes, rhs_scale=rhs_scales, start=True, stop=True)
 
-        rem_sg = sbt("rem_sg", [P, I], U8)
         rem_wg = sbt("rem_wg", [P, I], U16)
-        nc.vector.tensor_copy(rem_sg[:], rem_s[:].indirect(slots[:]))
-        q_mx = quantise("q", weave(nc.scalar.copy, "q_woven", q_raw, Q), Q)
         nc.vector.tensor_copy(rem_wg[:], rem_w[:].indirect(slots[:]))
-        c_woven = [weave(copy, "c_woven%d" % ch, c_raw[ch], UC) for ch, copy in enumerate((nc.scalar.copy, nc.vector.tensor_copy))]
+        rem_sg = sbt("rem_sg", [P, I], U8)
+        nc.vector.tensor_copy(rem_sg[:], rem_s[:].indirect(slots[:]))
+        c_woven = [weave(nc.vector.tensor_copy, "c_woven0", c_raw[0], UC, "rem_w")]
+        q_mx = quantise("q", weave(nc.scalar.copy, "q_woven", q_raw, Q), Q, "rem_s")
+        c_woven.append(weave(nc.vector.tensor_copy, "c_woven1", c_raw[1], UC, "q_woven"))
+        c_mx = [quantise("c%d" % ch, c_woven[ch], UC) for ch in range(CH)]
+
+        def centre_scores(h, ch):
+            mx(bank[2 * ch + h][:, :UC], q_mx, slice(h * P, (h + 1) * P), c_mx[ch][0][:].bitcast(FP8X4), c_mx[ch][1][:])
+            nc.scalar.copy(c1[h][:, ch * UC : (ch + 1) * UC], bank[2 * ch + h][:, :UC])
 
         b_sb = [sbt("b_sb%d" % h, [P, I], F32) for h in range(QT)]
         for h in range(QT):
             mx(bank[4 + h][:], q_mx, slice(h * P, (h + 1) * P), rem_wg[:].bitcast(FP4X4), rem_sg[:])
             nc.scalar.copy(b_sb[h][:], bank[4 + h][:])
-        for ch in range(CH):
-            c_mx = quantise("c%d" % ch, c_woven[ch], UC)
-            for h in range(QT):
-                mx(bank[2 * ch + h][:, :UC], q_mx, slice(h * P, (h + 1) * P), c_mx[0][:].bitcast(FP8X4), c_mx[1][:])
-                nc.scalar.copy(c1[h][:, ch * UC : (ch + 1) * UC], bank[2 * ch + h][:, :UC])
+        for h in range(QT):
+            for ch in range(CH):
+                centre_scores(h, ch)
 
         size_row = sbt("size_row", [P, I], F32)
         for t in range(PACK):
-            nc.tensor.transpose(bank[3][:, t * P : (t + 1) * P], size4[:, t : t + 1].to_broadcast([P, P]), ident[:])
+            nc.tensor.transpose(bank[7][:, t * P : (t + 1) * P], size4[:, t : t + 1].to_broadcast([P, P]), ident[:])
         nc.scalar.copy(size_row[:].rearrange("c (u b r t) -> c u b r t", u=2, b=16, r=4),
-                       bank[3][:].rearrange("c (t b u r) -> c u b r t", t=4, b=16, u=2))
+                       bank[7][:].rearrange("c (t b u r) -> c u b r t", t=4, b=16, u=2))
 
-        def turn(name, half_words, bk, tag=None):
+        def turn(name, half_words, bk):
             words = half_words[:].bitcast(F32)
             for u in range(2):
                 nc.tensor.transpose(bk[:, u * P : (u + 1) * P], words[:, u * P : (u + 1) * P], ident[:])
             woven = sbt(name + "_woven", [P, P * PACK], BF16)
             nc.scalar.copy(woven[:].bitcast(F32).rearrange("p (c u) -> p c u", u=2),
                            bk[:, : 2 * P].rearrange("p (u c) -> p c u", u=2))
-            return quantise(name, woven[:], P, tag)
+            return woven[:]
 
-        s = [sbt("s%d" % h, [P, I], F32) for h in range(QT)]
+
         neg_max = [sbt("neg_max%d" % h, [P, 1], F32) for h in range(QT)]
-        p_exp = [sbt("p_exp%d" % h, [P, I], F32) for h in range(QT)]
         total = sbt("total", [P, QT], F32)
         inv = sbt("inv", [P, QT], F32)
         w = [sbt("w%d" % h, [P, I], BF16) for h in range(QT)]
-        vg_tag = ["vg0", "b_sb1", "p_exp0", "vg3"]
-        vg = []
+        vg = {}
 
-        def gather_values(j):
-            vg.append(sbt("vg%d" % j, [P, I], BF16, vg_tag[j]))
-            nc.vector.tensor_copy(vg[j][:].rearrange("p (u b r) -> p b u r", u=2, b=16), v_raw[j][:].indirect(slots[:]))
+        def dealt(t):
+            return t[:].rearrange("p (u b r) -> p b u r", u=2, b=16)
 
-        gather_values(0)
-        for h in range(QT):
-            nc.vector.tensor_tensor(s[h][:], c1[h][:].indirect(centres[:]), b_sb[h][:], ALU.add)
-        for h in range(QT):
-            nc.vector.tensor_reduce(neg_max[h][:], s[h][:], mybir.AxisListType.X, ALU.max, negate=True)
-            nc.scalar.activation(p_exp[h][:].rearrange("p (u b r) -> p u b r", u=2, b=16),
-                                 s[h][:].rearrange("p (b u r) -> p u b r", u=2, b=16),
-                                 ACT.Exp, bias=neg_max[h][:], accum_out=total[:, h : h + 1])
+        def gather_values(j, tag):
+            vg[j] = sbt("vg%d" % j, [P, I], BF16, tag)
+            nc.vector.tensor_copy(dealt(vg[j]), v_raw[j][:].indirect(slots[:]))
+
         v_bank = [bank[6], bank[7], bank[2], bank[3]]
-        v_mx = []
-        w_mx = []
-        gather_values(1)
+        gather_values(0, "q_woven")
+        v_woven = {0: turn("v0", vg[0], v_bank[0])}
+        v1_half = sbt("v1_half", [P, T], BF16)
+        nc.scalar.activation(v1_half[:], v_raw[1][:], ACT.Copy)
+        scores = sbt("scores", [P, QT, I], F32, "v_raw0")
+        s = [scores[:, h, :] for h in range(QT)]
+        p_exp = [sbt("p_exp0", [P, I], F32, "v_raw1"), sbt("p_exp1", [P, I], F32)]
+        for h in range(QT):
+            nc.vector.tensor_tensor(s[h], c1[h][:].indirect(centres[:]), b_sb[h][:], ALU.add)
+        for h in range(QT):
+            nc.vector.tensor_reduce(neg_max[h][:], s[h], mybir.AxisListType.X, ALU.max, negate=True)
+            nc.scalar.activation(p_exp[h][:].rearrange("p (u b r) -> p u b r", u=2, b=16),
+                                 s[h].rearrange("p (b u r) -> p u b r", u=2, b=16),
+                                 ACT.Exp, bias=neg_max[h][:], accum_out=total[:, h : h + 1])
+        vg[1] = sbt("vg1", [P, I], BF16, "neg_max0")
+        nc.scalar.activation(dealt(vg[1]), v1_half[:].indirect(slots[:]), ACT.Copy)
+        gather_values(2, "b_sb1")
         nc.vector.reciprocal(inv[:], total[:])
-        v_mx.append(turn("v0", vg[0], v_bank[0], "s1"))
+        v_mx = {0: quantise("v0", v_woven[0], P, "neg_max1")}
         for h in range(QT):
             nc.vector.scalar_tensor_tensor(w[h][:], p_exp[h][:], inv[:, h : h + 1], size_row[:], ALU.mult, ALU.mult)
-        gather_values(2)
-        v_mx.append(turn("v1", vg[1], v_bank[1]))
-        for h in range(QT):
-            w_mx.append(turn("w%d" % h, w[h], bank[4 + h]))
-        gather_values(3)
+        gather_values(3, "v_raw1")
+        v_woven[2] = turn("v2", vg[2], v_bank[2])
+        w_woven = [turn("w0", w[0], bank[4])]
+        v_woven[1] = turn("v1", vg[1], v_bank[1])
+        w_woven.append(turn("w1", w[1], bank[5]))
+        v_woven[3] = turn("v3", vg[3], v_bank[3])
+        late = sbt("late_codes", [P, 4, P], U32, "v_raw3")
+        w_mx = [quantise("w%d" % h, w_woven[h], P, codes=late[:, h, :]) for h in range(QT)]
+        for n, j in enumerate((2, 1)):
+            v_mx[j] = quantise("v%d" % j, v_woven[j], P, codes=late[:, 2 + n, :])
+        v_mx[3] = quantise("v3", v_woven[3], P)
 
         o_bank = [bank[h][:].rearrange("p (j q) -> p j q", j=PACK) for h in range(QT)]
         o_sb = sbt("o_sb", [P, PACK, Q], F32)
-        out_v = out_0.rearrange("(p j) q -> p j q", j=PACK)
-
-        def product(j):
+        for j in (0, 2, 1, 3):
             for h in range(QT):
                 mx(o_bank[h][:, j, :], v_mx[j], slice(0, P), w_mx[h][0][:].bitcast(FP8X4), w_mx[h][1][:])
-
-        product(0)
-        product(1)
-        for h in range(QT):
-            nc.scalar.copy(o_sb[:, :2, h * P : (h + 1) * P], o_bank[h][:, :2, :])
-        nc.sync.dma_start(out_v[:, :2, :], o_sb[:, :2, :])
-        v_mx.append(turn("v2", vg[2], v_bank[2], "v_raw3"))
-        product(2)
-        v_mx.append(turn("v3", vg[3], v_bank[3]))
-        product(3)
 
         o_woven = sbt("o_woven", [P, Q, PACK], BF16)
         nc.scalar.copy(o_woven[:, :P, :], o_bank[0].rearrange("p j q -> p q j"))
         nc.vector.tensor_copy(o_woven[:, P:, :], o_bank[1].rearrange("p j q -> p q j"))
-        for h in range(QT):
-            nc.scalar.copy(o_sb[:, 2:, h * P : (h + 1) * P], o_bank[h][:, 2:, :])
-        nc.scalar.dma_start(out_v[:, 2:, :], o_sb[:, 2:, :])
+        nc.scalar.copy(o_sb[:, :, :P], o_bank[0])
+        nc.vector.tensor_copy(o_sb[:, :, P:], o_bank[1])
+        nc.sync.dma_start(out_0.rearrange("(p j) q -> p j q", j=PACK), o_sb[:])
         o_codes, o_scales = quantise("o", o_woven[:].rearrange("p c t -> p (c t)"), Q)
-        nc.sync.dma_start(out_1[0].rearrange("p c t -> p (c t)").bitcast(I32), o_codes[:].bitcast(I32))
+        nc.scalar.dma_start(out_1[0].rearrange("p c t -> p (c t)").bitcast(I32), o_codes[:].bitcast(I32))
         for g in range(4):
             eng = nc.sync if g < 2 else nc.scalar
             eng.dma_start(out_2[0, 4 * g : 4 * g + 4, :].bitcast(I32), o_scales[32 * g : 32 * g + 4, :].bitcast(I32))

from contextlib import ExitStack

import concourse.mybir as mybir
from concourse.masks import make_identity

D, T, I, Q, E, U = 512, 2048, 512, 256, 512, 512
FLOPS = 2 * D * Q * U + 2 * D * Q * I + 2 * I * E * Q

F32 = mybir.dt.float32
BF16 = mybir.dt.bfloat16
I32 = mybir.dt.int32
U32 = mybir.dt.uint32
U16 = mybir.dt.uint16
U8 = mybir.dt.uint8
FP8X4 = mybir.dt.float8_e4m3fn_x4
FP4X4 = mybir.dt.float4_e2m1fn_x4
ALU = mybir.AluOpType
ACT = mybir.ActivationFunctionType

P = 128
PACK = 4
QT = Q // P
CH = 2
UC = U // CH
SPARE = 16


def tile_attend_centreremainder_pl_kernel(tc, query, cent, rem_words, rem_scales, size, vals, offs, offs2, out_0, out_1, out_2):
    nc = tc.nc
    with ExitStack() as ctx:
        sb = ctx.enter_context(tc.tile_pool(name="sb", bufs=1))
        ps = ctx.enter_context(tc.psum_pool(name="ps", bufs=1))

        def sbt(name, shape, dt, tag=None):
            return sb.tile(shape, dt, name=name, tag=tag or name, align_bytes=64)

        slots = sbt("slots", [P, I // 16], U16)
        centres = sbt("centres", [P, I // 16], U16)
        bank = [ps.tile([P, 512], F32, name="bank%d" % b) for b in range(8)]

        rem_w = sbt("rem_w", [P, T], U16)
        rem_s = sbt("rem_s", [P, T], U8)
        q_raw = sbt("q_raw", [P, PACK, Q], F32)
        c_raw = [sbt("c_raw%d" % h, [P, PACK, UC], F32) for h in range(CH)]
        size4 = sbt("size4", [P, PACK], F32)
        v_raw = [sbt("v_raw%d" % j, [P, T], F32) for j in range(PACK)]
        c1 = [sbt("c1_%d" % h, [P, U + SPARE], F32) for h in range(QT)]
        ident = sbt("ident", [P, P], F32)

        nc.gpsimd.memset(rem_s[:].bitcast(I32), 0)
        nc.sync.dma_start(slots[:], offs)
        nc.sync.dma_start(rem_w[:].bitcast(I32), rem_words[0].bitcast(I32))
        nc.sync.dma_start(q_raw[:], query.rearrange("(p j) q -> p j q", j=PACK))
        cent_v = cent.rearrange("(p j) u -> p j u", j=PACK)
        nc.sync.dma_start(size4[:], size.rearrange("o (p t) -> p (o t)", t=PACK))
        for g in range(4):
            nc.sync.dma_start(rem_s[32 * g : 32 * g + 4, :].bitcast(I32), rem_scales[0, 4 * g : 4 * g + 4, :].bitcast(I32))
        nc.sync.dma_start(c_raw[0][:], cent_v[:, :, :UC])
        nc.sync.dma_start(c_raw[1][:], cent_v[:, :, UC:])
        nc.sync.dma_start(centres[:], offs2)
        vals_v = vals.rearrange("(p j) t -> j p t", j=PACK)
        for j in range(PACK):
            nc.sync.dma_start(v_raw[j][:], vals_v[j])

        make_identity(nc, ident[:])
        for h in range(QT):
            nc.gpsimd.memset(c1[h][:, U:], 0.0)

        def weave(copy, name, raw, width, tag=None):
            woven = sbt(name, [P, width, PACK], BF16, tag)
            copy(woven[:].rearrange("p (c i) t -> p c t i", i=4), raw[:].rearrange("p t (c i) -> p c t i", i=4))
            return woven[:].rearrange("p c t -> p (c t)")

        def quantise(name, woven, width, tag=None, codes=None):
            if codes is None:
                codes = sbt(name + "_codes", [P, width], U32, tag)
            scales = sbt(name + "_scales", [P, width], U8)
            nc.vector.quantize_mx(out=codes[:].bitcast(FP8X4), scales=scales[:], in_=woven)
            return codes, scales

        def mx(out, lhs, lcols, rhs_codes, rhs_scales):
            nc.tensor.matmul_mx(out=out, lhsT=lhs[0][:, lcols].bitcast(FP8X4), lhsT_scale=lhs[1][:, lcols],
                                rhs=rhs_codes, rhs_scale=rhs_scales, start=True, stop=True)

        rem_wg = sbt("rem_wg", [P, I], U16)
        nc.vector.tensor_copy(rem_wg[:], rem_w[:].indirect(slots[:]))
        rem_sg = sbt("rem_sg", [P, I], U8)
        nc.vector.tensor_copy(rem_sg[:], rem_s[:].indirect(slots[:]))
        c_woven = [weave(nc.vector.tensor_copy, "c_woven0", c_raw[0], UC, "rem_w")]
        q_mx = quantise("q", weave(nc.scalar.copy, "q_woven", q_raw, Q), Q, "rem_s")
        c_woven.append(weave(nc.vector.tensor_copy, "c_woven1", c_raw[1], UC, "q_woven"))
        c_mx = [quantise("c%d" % ch, c_woven[ch], UC) for ch in range(CH)]

        def centre_scores(h, ch):
            mx(bank[2 * ch + h][:, :UC], q_mx, slice(h * P, (h + 1) * P), c_mx[ch][0][:].bitcast(FP8X4), c_mx[ch][1][:])
            nc.scalar.copy(c1[h][:, ch * UC : (ch + 1) * UC], bank[2 * ch + h][:, :UC])

        b_sb = [sbt("b_sb%d" % h, [P, I], F32) for h in range(QT)]
        for h in range(QT):
            mx(bank[4 + h][:], q_mx, slice(h * P, (h + 1) * P), rem_wg[:].bitcast(FP4X4), rem_sg[:])
            nc.scalar.copy(b_sb[h][:], bank[4 + h][:])
        for h in range(QT):
            for ch in range(CH):
                centre_scores(h, ch)

        size_row = sbt("size_row", [P, I], F32)
        for t in range(PACK):
            nc.tensor.transpose(bank[7][:, t * P : (t + 1) * P], size4[:, t : t + 1].to_broadcast([P, P]), ident[:])
        nc.scalar.copy(size_row[:].rearrange("c (u b r t) -> c u b r t", u=2, b=16, r=4),
                       bank[7][:].rearrange("c (t b u r) -> c u b r t", t=4, b=16, u=2))

        def turn(name, half_words, bk):
            words = half_words[:].bitcast(F32)
            for u in range(2):
                nc.tensor.transpose(bk[:, u * P : (u + 1) * P], words[:, u * P : (u + 1) * P], ident[:])
            woven = sbt(name + "_woven", [P, P * PACK], BF16)
            nc.scalar.copy(woven[:].bitcast(F32).rearrange("p (c u) -> p c u", u=2),
                           bk[:, : 2 * P].rearrange("p (u c) -> p c u", u=2))
            return woven[:]


        neg_max = [sbt("neg_max%d" % h, [P, 1], F32) for h in range(QT)]
        total = sbt("total", [P, QT], F32)
        inv = sbt("inv", [P, QT], F32)
        w = [sbt("w%d" % h, [P, I], BF16) for h in range(QT)]
        vg = {}

        def dealt(t):
            return t[:].rearrange("p (u b r) -> p b u r", u=2, b=16)

        def gather_values(j, tag):
            vg[j] = sbt("vg%d" % j, [P, I], BF16, tag)
            nc.vector.tensor_copy(dealt(vg[j]), v_raw[j][:].indirect(slots[:]))

        v_bank = [bank[6], bank[7], bank[2], bank[3]]
        gather_values(0, "q_woven")
        v_woven = {0: turn("v0", vg[0], v_bank[0])}
        v1_half = sbt("v1_half", [P, T], BF16)
        nc.scalar.activation(v1_half[:], v_raw[1][:], ACT.Copy)
        scores = sbt("scores", [P, QT, I], F32, "v_raw0")
        s = [scores[:, h, :] for h in range(QT)]
        p_exp = [sbt("p_exp0", [P, I], F32, "v_raw1"), sbt("p_exp1", [P, I], F32)]
        for h in range(QT):
            nc.vector.tensor_tensor(s[h], c1[h][:].indirect(centres[:]), b_sb[h][:], ALU.add)
        for h in range(QT):
            nc.vector.tensor_reduce(neg_max[h][:], s[h], mybir.AxisListType.X, ALU.max, negate=True)
            nc.scalar.activation(p_exp[h][:].rearrange("p (u b r) -> p u b r", u=2, b=16),
                                 s[h].rearrange("p (b u r) -> p u b r", u=2, b=16),
                                 ACT.Exp, bias=neg_max[h][:], accum_out=total[:, h : h + 1])
        vg[1] = sbt("vg1", [P, I], BF16, "neg_max0")
        nc.scalar.activation(dealt(vg[1]), v1_half[:].indirect(slots[:]), ACT.Copy)
        gather_values(2, "b_sb1")
        nc.vector.reciprocal(inv[:], total[:])
        v_mx = {0: quantise("v0", v_woven[0], P, "neg_max1")}
        for h in range(QT):
            nc.vector.scalar_tensor_tensor(w[h][:], p_exp[h][:], inv[:, h : h + 1], size_row[:], ALU.mult, ALU.mult)
        gather_values(3, "v_raw1")
        v_woven[2] = turn("v2", vg[2], v_bank[2])
        w_woven = [turn("w0", w[0], bank[4])]
        v_woven[1] = turn("v1", vg[1], v_bank[1])
        w_woven.append(turn("w1", w[1], bank[5]))
        v_woven[3] = turn("v3", vg[3], v_bank[3])
        late = sbt("late_codes", [P, 4, P], U32, "v_raw3")
        w_mx = [quantise("w%d" % h, w_woven[h], P, codes=late[:, h, :]) for h in range(QT)]
        for n, j in enumerate((2, 1)):
            v_mx[j] = quantise("v%d" % j, v_woven[j], P, codes=late[:, 2 + n, :])
        v_mx[3] = quantise("v3", v_woven[3], P)

        o_bank = [bank[h][:].rearrange("p (j q) -> p j q", j=PACK) for h in range(QT)]
        o_sb = sbt("o_sb", [P, PACK, Q], F32)
        for j in (0, 2, 1, 3):
            for h in range(QT):
                mx(o_bank[h][:, j, :], v_mx[j], slice(0, P), w_mx[h][0][:].bitcast(FP8X4), w_mx[h][1][:])

        o_woven = sbt("o_woven", [P, Q, PACK], BF16)
        nc.scalar.copy(o_woven[:, :P, :], o_bank[0].rearrange("p j q -> p q j"))
        nc.vector.tensor_copy(o_woven[:, P:, :], o_bank[1].rearrange("p j q -> p q j"))
        nc.scalar.copy(o_sb[:, :, :P], o_bank[0])
        nc.vector.tensor_copy(o_sb[:, :, P:], o_bank[1])
        nc.sync.dma_start(out_0.rearrange("(p j) q -> p j q", j=PACK), o_sb[:])
        o_codes, o_scales = quantise("o", o_woven[:].rearrange("p c t -> p (c t)"), Q)
        nc.scalar.dma_start(out_1[0].rearrange("p c t -> p (c t)").bitcast(I32), o_codes[:].bitcast(I32))
        for g in range(4):
            eng = nc.sync if g < 2 else nc.scalar
            eng.dma_start(out_2[0, 4 * g : 4 * g + 4, :].bitcast(I32), o_scales[32 * g : 32 * g + 4, :].bitcast(I32))
